import numpy as np
import ml_dtypes


def mxq(x, axis, fmt="e4m3"):
    dtype, down = {"e4m3": (ml_dtypes.float8_e4m3fn, 7), "e5m2": (ml_dtypes.float8_e5m2, 14)}[fmt]
    v = np.moveaxis(np.asarray(x, np.float32).astype(ml_dtypes.bfloat16).astype(np.float64), axis, -1)
    blocks = v.reshape(v.shape[:-1] + (-1, 32))
    amax = np.abs(blocks).max(-1, keepdims=True)
    byte = np.maximum(np.where(amax > 0, np.frexp(amax)[1] - 1 + 127, 0) - down, 1)
    scale = np.exp2(byte - 127.0)
    codes = (blocks / scale).astype(np.float32).astype(dtype).astype(np.float64)
    return np.moveaxis((codes * scale).reshape(v.shape), -1, axis)


WIDE = False


def mx_kscale(k):
    if not WIDE:
        return np.ones(k)
    levels = np.array([10, -10, 5, -5, 0])
    if k % 512:
        return np.exp2(np.random.permutation(np.resize(levels, k // 32))).repeat(32)
    a = np.empty((k // 512, 16))
    for p in range(k // 512):
        a[p, :8] = np.random.permutation(np.resize(levels, 8))
        for g in range(8):
            far = levels[np.abs(levels - a[p, g]) >= 10]
            a[p, g + 8] = far[np.random.randint(len(far))]
    return np.exp2(a.ravel()).repeat(32)


BF16 = ml_dtypes.bfloat16


def bf(x):
    return np.asarray(x, np.float32).astype(BF16)


def f64(x):
    return np.asarray(x).astype(np.float64)


T, K, F, Q = 2048, 1024, 512, 1024


def draw0():
    s, t = mx_kscale(K), mx_kscale(T)
    loudness = np.exp(0.7 * np.random.standard_normal((T, 1)))
    return {"power": bf(np.exp(np.random.standard_normal((T, K)) - 0.5) * loudness * s),
            "filters": bf(np.exp(2.0 * np.random.standard_normal((K, F)) - 2.0) / K / s[:, None]),
            "offset": bf(0.1 + 0.4 * np.random.random(F)),
            "gain": bf(1.0 + 0.1 * np.random.standard_normal(F)),
            "bias": bf(0.3 * np.random.standard_normal(F)),
            "frame_weight": bf((0.5 + 0.5 * np.random.random(T)) * t),
            "basis": bf(np.random.standard_normal((Q, T)) / np.sqrt(T) / t),
            "lifter": bf(1.0 + 0.1 * np.random.standard_normal(Q))}


def core(power, filters, offset, gain, bias, frame_weight, basis, lifter):
    e = mxq(f64(power), 1, "e4m3") @ mxq(f64(filters), 0, "e4m3")
    y = f64(gain) * np.log(e + f64(offset)) + f64(bias)
    h = f64(frame_weight)[:, None] * y
    c = mxq(f64(basis), 1, "e4m3") @ mxq(h, 0, "e4m3")
    return f64(lifter)[:, None] * c


def e4m3fn_bytes(y):
    return np.clip(np.asarray(y, np.float64), -448.0, 448.0).astype(np.float32).astype(ml_dtypes.float8_e4m3fn).view(np.uint8)


def e4m3fn_values(b):
    return np.asarray(b, np.uint8).view(ml_dtypes.float8_e4m3fn).astype(np.float64)


def setup_inputs():
    d = draw0()
    x0 = np.asarray(d['power']).astype(np.float64)
    s = (np.max(np.abs(x0), axis=(0,), keepdims=True) / 448.0).astype(np.float32)
    out = {}
    for k, v in d.items():
        if k == 'power':
            out['power_bytes'] = e4m3fn_bytes(x0 / s.astype(np.float64))
            out['power_scale'] = s
        else:
            out[k] = v
    return out


def reference(power_bytes, power_scale, filters, offset, gain, bias, frame_weight, basis, lifter):
    return core(e4m3fn_values(power_bytes) * power_scale.astype(np.float64), filters, offset, gain, bias, frame_weight, basis, lifter)

@@ -1,0 +1,336 @@
+from contextlib import ExitStack
+
+import concourse.mybir as mybir
+from concourse.masks import make_identity
+
+T, K, F, Q = 2048, 1024, 512, 1024
+FLOPS = 2 * T * K * F + 2 * Q * T * F
+
+STEPS = """
+st0:p rowsf:v st1:p sev0:v sev1:s btr51:p prod03:v bev51:s prod02:v fil01:s prod01:v ptr010:p
+fil00:s prod00:v fil10:s prod13:v pev010:s fil11:s prod12:v btr10:p ptr000:p prod10:v bev10:s
+ptr011:p pev000:s ptr001:p prod11:v pev011:s btr11:p pev001:s btr30:p prod23:v bev11:s ptr100:p
+bev30:s btr20:p prod22:v pev100:s ptr110:p bev20:s ptr101:p prod21:v pev110:s ptr211:p pev101:s
+ptr111:p prod20:v pev211:s btr00:p pev111:s ptr210:p pq00:v bev00:s ptr201:p fq0:v pev210:s btr01:p
+fq1:v pev201:s btr21:p pq01:v bev01:s btr50:p prod33:v bev21:s pt:p mx100:p bev50:s mx101:p cols:v
+prod30:v ln00:s ptr200:p ln01:s btr31:p prod31:v pev200:s mx103:p gb00:s pq11:v mx102:p ln03:s
+ptr300:p pq10:v ln02:s prod32:v ptr301:p bev31:s mx113:p pev301:s pq20:v mx110:p pev300:s gb03:v
+ptr311:p ln13:s pq21:v ptr310:p ln10:s bq5:v btr41:p pev311:s gb02:v mx111:p gb01:v pev310:s bq1:v
+mx112:p ln11:s bq3:v btr40:p bev41:s pq30:v htr00:p bev40:s htr01:p hex00:v mx123:p ln12:s hex01:v
+htr02:p ln23:s pq31:v htr03:p btr71:p gb13:s gb23:v hex02:v mx122:p gb12:s hex03:v bev71:s mx121:p
+gb10:v ln22:s htr13:p bq0:v btr70:p ln21:s hex13:v btr60:p bev70:s gb11:v htr12:p bq2:v gb21:s
+htr23:p mx120:p hq0:v bev60:s hex12:v mx130:p ln20:s htr10:p hex23:v gb22:s htr11:p hex10:v htr21:p
+gb20:s mx132:p hex11:v ln30:s htr22:p hex21:v ln32:s htr20:p hex22:v btr61:p gb32:s hex20:v mx133:p
+gb30:s hq1:v mx131:p ln33:s hq2:v htr32:p bev61:s htr30:p gb33:v mx23_0:p hex32:v ln31:s gb31:v
+htr33:p hex30:v oev3_0:s htr31:p hex33:v mx22_0:p hex31:v mx21_0:p bq4:v oev2_0:s hq3:v mx20_0:p
+oev1_0:s bq6:v mx22_1:p oev0_0:s mx24_0:p oev2_1:v bq7:v mx21_1:p mx25_0:p oev4_0:v oev1_1:v
+mx23_1:p oev5_0:v mx26_0:p oev3_1:v mx20_1:p oev6_0:v mx27_0:p oev0_1:v oev7_0:v
+"""
+
+P = 128
+SPLIT = [[[0, 1, 2], [3]]] * 4 + [[[0, 1, 2, 3]]] * 4
+GROUPS = T // 512
+PASSES = K // 512
+FB = F // P
+QT = Q // P
+
+F32 = mybir.dt.float32
+BF16 = mybir.dt.bfloat16
+U32 = mybir.dt.uint32
+U8 = mybir.dt.uint8
+FP8 = mybir.dt.float8_e4m3fn
+FP8X4 = mybir.dt.float8_e4m3fn_x4
+ALU = mybir.AluOpType
+ACT = mybir.ActivationFunctionType
+
+
+def tile_temporal_log_mel_cepstrum_f4_kernel(
+    tc, power_bytes, power_scale, filters, offset, gain, bias, frame_weight, basis, lifter, out
+):
+    nc = tc.nc
+    with ExitStack() as ctx:
+        const = ctx.enter_context(tc.tile_pool(name="const", bufs=1))
+        keep = ctx.enter_context(tc.tile_pool(name="keep", bufs=1))
+        work = ctx.enter_context(tc.tile_pool(name="work", bufs=2))
+        tr_pool = ctx.enter_context(tc.psum_pool(name="tr", bufs=3))
+        e_pool = ctx.enter_context(tc.psum_pool(name="epool", bufs=2))
+        c_pool = ctx.enter_context(tc.psum_pool(name="cpool", bufs=3))
+        ctx.enter_context(tc.manual_schedule())
+
+        ident = const.tile([P, P], F32, name="ident")
+        warm = const.tile([P, 1], F32, name="warm")
+        warm_out = const.tile([P, 1], F32, name="warm_out")
+        s_col = const.tile([P, 8], F32, name="s_col")
+        s_row = const.tile([P, K], F32, name="s_row")
+        rows_bf = const.tile([P, P], BF16, name="rows_bf")
+        rows_f = const.tile([P, P], F32, name="rows_f")
+        cols = const.tile([P, 20], F32, name="cols")
+        fw = const.tile([P, GROUPS, 4], BF16, name="fw")
+
+        code_in = [keep.tile([P, 4, K], U8, name="code_in%d" % g) for g in range(GROUPS)]
+        f_raw = [keep.tile([P, 4, F], BF16, name="f_raw%d" % s) for s in range(PASSES)]
+        f_il = [keep.tile([P, F, 4], BF16, name="f_il%d" % s, align_bytes=64) for s in range(PASSES)]
+        f_codes = [keep.tile([P, F], U32, name="f_codes%d" % s, align_bytes=64) for s in range(PASSES)]
+        f_scales = [keep.tile([P, F], U8, name="f_scales%d" % s, align_bytes=64) for s in range(PASSES)]
+        b_raw = [keep.tile([P, T], BF16, name="b_raw%d" % q) for q in range(QT)]
+        b_codes = [keep.tile([P, 512], U32, name="b_codes%d" % q, align_bytes=64) for q in range(QT)]
+        b_scales = [keep.tile([P, 512], U8, name="b_scales%d" % q, align_bytes=64) for q in range(QT)]
+        h_codes = [keep.tile([P, F], U32, name="h_codes%d" % g, align_bytes=64) for g in range(GROUPS)]
+        h_scales = [keep.tile([P, F], U8, name="h_scales%d" % g, align_bytes=64) for g in range(GROUPS)]
+
+        p_src = power_bytes.rearrange("(g p t) k -> g p t k", p=P, t=4)
+        f_src = filters.rearrange("(s p j) w -> s p j w", p=P, j=4)
+        b_src = basis.rearrange("(q p) t -> q p t", p=P)
+
+        def load(dst, src):
+            nc.sync.dma_start(out=dst, in_=src)
+
+        nc.vector.memset(rows_bf[:], 0.0)
+        nc.vector.memset(warm[:], 1.0)
+        make_identity(nc, ident[:])
+        nc.scalar.activation(out=warm_out[:], in_=warm[:], func=ACT.Ln)
+
+        load(s_col[:], power_scale.rearrange("o (p j) -> p (o j)", p=P))
+        load(rows_bf[0:4, :], offset.rearrange("(c p) -> c p", p=P))
+        load(rows_bf[4:8, :], gain.rearrange("(c p) -> c p", p=P))
+        load(rows_bf[8:12, :], bias.rearrange("(c p) -> c p", p=P))
+        load(rows_bf[12:20, :], lifter.rearrange("(c p) -> c p", p=P))
+        load(b_raw[5][:], b_src[5])
+        load(code_in[0][:, 2:4, :], p_src[0][:, 2:4, :])
+        load(f_raw[0][:], f_src[0])
+        load(code_in[0][:, 0:2, :], p_src[0][:, 0:2, :])
+        load(f_raw[1][:], f_src[1])
+        load(code_in[1][:, 2:4, :], p_src[1][:, 2:4, :])
+        load(code_in[2][:, 2:4, :], p_src[2][:, 2:4, :])
+        load(code_in[1][:, 0:2, :], p_src[1][:, 0:2, :])
+        load(fw[:], frame_weight.rearrange("(g p t) -> p g t", p=P, t=4))
+        load(b_raw[1][:], b_src[1])
+        load(b_raw[4][:], b_src[4])
+        load(b_raw[3][:], b_src[3])
+        load(code_in[2][:, 0:2, :], p_src[2][:, 0:2, :])
+        load(b_raw[2][:], b_src[2])
+        load(b_raw[0][:], b_src[0])
+        load(code_in[3][:, 2:4, :], p_src[3][:, 2:4, :])
+        load(code_in[3][:, 0:2, :], p_src[3][:, 0:2, :])
+        load(b_raw[6][:], b_src[6])
+        load(b_raw[7][:], b_src[7])
+
+        x_tiles, p_tr, p_il, p_codes, p_scales = {}, {}, {}, {}, {}
+        b_tr, b_il = {}, {}
+        e_acc, l_tiles, y_tiles, h_tr, h_il = {}, {}, {}, {}, {}
+        c_acc = {}
+
+        st_t = {}
+
+        def scale_tr(half):
+            st = tr_pool.tile([P, 4, P], F32, name="st", tag="tr")
+            st_t[half] = st
+            for j in range(4):
+                jj = 4 * half + j
+                nc.tensor.transpose(st[:, j, :], s_col[:, jj : jj + 1].to_broadcast([P, P]), ident[:])
+
+        def copy(eng, dst, src):
+            if eng == "v":
+                nc.vector.tensor_copy(out=dst, in_=src)
+            else:
+                nc.scalar.copy(out=dst, in_=src)
+
+        def scale_ev(half, eng):
+            dst = s_row[:].rearrange("p (n j) -> p n j", j=8)[:, :, 4 * half : 4 * half + 4]
+            copy(eng, dst, st_t[half][:].rearrange("p j n -> p n j"))
+
+        def par(step):
+            if step == 0:
+                nc.vector.tensor_copy(out=rows_f[:], in_=rows_bf[:])
+            elif step == 1:
+                pt = tr_pool.tile([P, P], F32, name="pt", tag="tr")
+                st_t["pt"] = pt
+                nc.tensor.transpose(pt[:], rows_f[:], ident[:])
+            else:
+                nc.vector.tensor_copy(out=cols[:], in_=st_t["pt"][:, 0:20])
+
+        def f_interleave(s, eng, lo, hi):
+            src = f_raw[s][:, :, lo:hi].rearrange("p j w -> p w j")
+            if eng == "v":
+                nc.vector.tensor_copy(out=f_il[s][:, lo:hi, :], in_=src)
+            else:
+                nc.scalar.copy(out=f_il[s][:, lo:hi, :], in_=src)
+
+        def f_quant(s):
+            nc.vector.quantize_mx(
+                out=f_codes[s][:].bitcast(FP8X4), scales=f_scales[s][:],
+                in_=f_il[s][:].rearrange("p w j -> p (w j)"))
+
+        def prod(g, t):
+            if g not in x_tiles:
+                x = work.tile([P, 4, K], BF16, name="x_bf", tag="x_bf", bufs=4)
+                x_tiles[g] = x
+            nc.vector.tensor_tensor(
+                out=x_tiles[g][:, t, :], in0=code_in[g][:, t, :].bitcast(FP8), in1=s_row[:], op=ALU.mult)
+
+        def ptr(g, tp, s):
+            pt = tr_pool.tile([P, 2, 2, P], F32, name="p_tr", tag="tr")
+            p_tr[g, tp, s] = pt
+            words = x_tiles[g][:].rearrange("p t k -> p (t k)").bitcast(F32)
+            for u in range(2):
+                for tt in range(2):
+                    base = 512 * (2 * tp + tt) + 256 * s
+                    nc.tensor.transpose(pt[:, u, tt, :], words[:, base + u : base + 256 : 2], ident[:])
+
+        def pev(g, tp, s, eng):
+            if (g, s) not in p_il:
+                il = work.tile([P, 512, 4], BF16, name="p_il", tag="p_il", bufs=5, align_bytes=64)
+                p_il[g, s] = il
+            words = p_il[g, s][:].rearrange("p n j -> p (n j)").bitcast(F32)
+            dst = words[:, 512 * tp : 512 * (tp + 1)].rearrange("p (n u) -> p n u", u=2)
+            copy(eng, dst, p_tr[g, tp, s][:].rearrange("p u t r -> p (t r) u"))
+
+        def pq(g, s):
+            codes = work.tile([P, 512], U32, name="p_codes", tag="p_codes", bufs=5, align_bytes=64)
+            scales = work.tile([P, 512], U8, name="p_scales", tag="p_scales", bufs=5, align_bytes=64)
+            p_codes[g, s], p_scales[g, s] = codes, scales
+            nc.vector.quantize_mx(out=codes[:].bitcast(FP8X4), scales=scales[:],
+                                  in_=p_il[g, s][:].rearrange("p n j -> p (n j)"))
+
+        def mx1(g, fb):
+            e = e_pool.tile([P, 512], F32, name="e_acc", tag="e")
+            e_acc[g, fb] = e
+            c = slice(P * fb, P * (fb + 1))
+            for s in range(PASSES):
+                nc.tensor.matmul_mx(
+                    out=e[:], lhsT=f_codes[s][:, c].bitcast(FP8X4), lhsT_scale=f_scales[s][:, c],
+                    rhs=p_codes[g, s][:].bitcast(FP8X4), rhs_scale=p_scales[g, s][:],
+                    start=(s == 0), stop=(s == PASSES - 1))
+
+        def ln(g, fb):
+            l = work.tile([P, 512], F32, name="l_t", tag="l_t", bufs=5)
+            l_tiles[g, fb] = l
+            nc.scalar.activation(out=l[:], in_=e_acc[g, fb][:], func=ACT.Ln, bias=cols[:, fb : fb + 1], scale=1.0)
+
+        def gb(g, fb, eng):
+            y = work.tile([P, 512], F32, name="y_t", tag="y_t", bufs=5)
+            y_tiles[g, fb] = y
+            gc, bc = cols[:, 4 + fb : 5 + fb], cols[:, 8 + fb : 9 + fb]
+            if eng == "v":
+                nc.vector.tensor_scalar(out=y[:], in0=l_tiles[g, fb][:], scalar1=gc, scalar2=bc, op0=ALU.mult, op1=ALU.add)
+            else:
+                nc.scalar.activation(out=y[:], in_=l_tiles[g, fb][:], func=ACT.Identity, bias=bc, scale=gc)
+
+        def htr(g, fb):
+            ht = tr_pool.tile([P, 4, P], F32, name="h_tr", tag="tr")
+            h_tr[g, fb] = ht
+            for t in range(4):
+                nc.tensor.transpose(ht[:, t, :], y_tiles[g, fb][:, P * t : P * (t + 1)], ident[:])
+
+        def hex_(g, fb):
+            if g not in h_il:
+                il = work.tile([P, F, 4], BF16, name="h_il", tag="h_il", bufs=2, align_bytes=64)
+                h_il[g] = il
+            nc.vector.tensor_tensor(
+                out=h_il[g][:, P * fb : P * (fb + 1), :], in0=h_tr[g, fb][:].rearrange("p t f -> p f t"),
+                in1=fw[:, g, :].unsqueeze(1).to_broadcast([P, P, 4]), op=ALU.mult)
+
+        def hq(g):
+            nc.vector.quantize_mx(out=h_codes[g][:].bitcast(FP8X4), scales=h_scales[g][:],
+                                  in_=h_il[g][:].rearrange("p f t -> p (f t)"))
+
+        def btr(q, h):
+            bt = tr_pool.tile([P, 2, 2, P], F32, name="b_tr", tag="tr")
+            b_tr[q, h] = bt
+            words = b_raw[q][:].bitcast(F32)
+            for gg in range(2):
+                for u in range(2):
+                    base = 256 * (2 * h + gg)
+                    nc.tensor.transpose(bt[:, gg, u, :], words[:, base + u : base + 256 : 2], ident[:])
+
+        def bev(q, h, eng):
+            if q not in b_il:
+                il = work.tile([P, 4, P, 4], BF16, name="b_il", tag="b_il", bufs=5, align_bytes=64)
+                b_il[q] = il
+            words = b_il[q][:].rearrange("p g q j -> p (g q j)").bitcast(F32)
+            dst = words[:, 512 * h : 512 * (h + 1)].rearrange("p (g q u) -> p g q u", g=2, u=2)
+            copy(eng, dst, b_tr[q, h][:].rearrange("p g u q -> p g q u"))
+
+        def bq(q):
+            nc.vector.quantize_mx(out=b_codes[q][:].bitcast(FP8X4), scales=b_scales[q][:],
+                                  in_=b_il[q][:].rearrange("p g q j -> p (g q j)"))
+
+        parts = {}
+
+        def mx2(q, i):
+            c = c_pool.tile([P, F], F32, name="c_acc", tag="c")
+            c_acc[q, i] = c
+            gs = SPLIT[q][i]
+            for g in gs:
+                cs = slice(P * g, P * (g + 1))
+                nc.tensor.matmul_mx(
+                    out=c[:], lhsT=b_codes[q][:, cs].bitcast(FP8X4), lhsT_scale=b_scales[q][:, cs],
+                    rhs=h_codes[g][:].bitcast(FP8X4), rhs_scale=h_scales[g][:],
+                    start=(g == gs[0]), stop=(g == gs[-1]))
+
+        def oev(q, i, eng):
+            last = i == len(SPLIT[q]) - 1
+            o = work.tile([P, F], F32, name="o_t", tag="o_t" if last else "part_t", bufs=4)
+            sc = cols[:, 12 + q : 13 + q]
+            src = c_acc[q, i]
+            if i > 0:
+                nc.vector.scalar_tensor_tensor(out=o[:], in0=src[:], scalar=sc, in1=parts[q][:], op0=ALU.mult, op1=ALU.add)
+            elif eng == "v":
+                nc.vector.tensor_scalar(out=o[:], in0=src[:], scalar1=sc, scalar2=None, op0=ALU.mult)
+            else:
+                nc.scalar.activation(out=o[:], in_=src[:], func=ACT.Copy, scale=sc)
+            parts[q] = o
+            if last:
+                nc.sync.dma_start(out=out[P * q : P * (q + 1), :], in_=o[:])
+
+        def run_step(name, eng):
+            if name.startswith("st"):
+                scale_tr(int(name[2:]))
+            elif name.startswith("sev"):
+                scale_ev(int(name[3:]), eng)
+            elif name == "rowsf":
+                par(0)
+            elif name == "pt":
+                par(1)
+            elif name == "cols":
+                par(2)
+            elif name.startswith("fil"):
+                h = int(name[4:])
+                f_interleave(int(name[3:4]), eng, 256 * h, 256 * h + 256)
+            elif name.startswith("fq"):
+                f_quant(int(name[2:]))
+            elif name.startswith("prod"):
+                prod(int(name[4:5]), int(name[5:]))
+            elif name.startswith("ptr"):
+                ptr(int(name[3:4]), int(name[4:5]), int(name[5:]))
+            elif name.startswith("pev"):
+                pev(int(name[3:4]), int(name[4:5]), int(name[5:]), eng)
+            elif name.startswith("pq"):
+                pq(int(name[2:3]), int(name[3:]))
+            elif name.startswith("mx1"):
+                mx1(int(name[3:4]), int(name[4:]))
+            elif name.startswith("ln"):
+                ln(int(name[2:3]), int(name[3:]))
+            elif name.startswith("gb"):
+                gb(int(name[2:3]), int(name[3:]), eng)
+            elif name.startswith("htr"):
+                htr(int(name[3:4]), int(name[4:]))
+            elif name.startswith("hex"):
+                hex_(int(name[3:4]), int(name[4:]))
+            elif name.startswith("hq"):
+                hq(int(name[2:]))
+            elif name.startswith("btr"):
+                btr(int(name[3:4]), int(name[4:]))
+            elif name.startswith("bev"):
+                bev(int(name[3:4]), int(name[4:]), eng)
+            elif name.startswith("bq"):
+                bq(int(name[2:]))
+            elif name.startswith("mx2"):
+                mx2(int(name[3:4]), int(name[5:]))
+            else:
+                assert name.startswith("oev")
+                oev(int(name[3:4]), int(name[5:]), eng)
+
+        for step in STEPS.split():
+            name, eng = step.split(":")
+            run_step(name, eng)

@@ -6,29 +6,31 @@ from concourse.masks import make_identity
 T, K, F, Q = 2048, 1024, 512, 1024
 FLOPS = 2 * T * K * F + 2 * Q * T * F
 
+PLAN = "ccceeppp"
+
 STEPS = """
-st0:p rowsf:v st1:p sev0:v sev1:s btr51:p prod03:v bev51:s prod02:v fil01:s prod01:v ptr010:p
-fil00:s prod00:v fil10:s prod13:v pev010:s fil11:s prod12:v btr10:p ptr000:p prod10:v bev10:s
-ptr011:p pev000:s ptr001:p prod11:v pev011:s btr11:p pev001:s btr30:p prod23:v bev11:s ptr100:p
-bev30:s btr20:p prod22:v pev100:s ptr110:p bev20:s ptr101:p prod21:v pev110:s ptr211:p pev101:s
-ptr111:p prod20:v pev211:s btr00:p pev111:s ptr210:p pq00:v bev00:s ptr201:p fq0:v pev210:s btr01:p
-fq1:v pev201:s btr21:p pq01:v bev01:s btr50:p prod33:v bev21:s pt:p mx100:p bev50:s mx101:p cols:v
-prod30:v ln00:s ptr200:p ln01:s btr31:p prod31:v pev200:s mx103:p gb00:s pq11:v mx102:p ln03:s
-ptr300:p pq10:v ln02:s prod32:v ptr301:p bev31:s mx113:p pev301:s pq20:v mx110:p pev300:s gb03:v
-ptr311:p ln13:s pq21:v ptr310:p ln10:s bq5:v btr41:p pev311:s gb02:v mx111:p gb01:v pev310:s bq1:v
-mx112:p ln11:s bq3:v btr40:p bev41:s pq30:v htr00:p bev40:s htr01:p hex00:v mx123:p ln12:s hex01:v
-htr02:p ln23:s pq31:v htr03:p btr71:p gb13:s gb23:v hex02:v mx122:p gb12:s hex03:v bev71:s mx121:p
-gb10:v ln22:s htr13:p bq0:v btr70:p ln21:s hex13:v btr60:p bev70:s gb11:v htr12:p bq2:v gb21:s
-htr23:p mx120:p hq0:v bev60:s hex12:v mx130:p ln20:s htr10:p hex23:v gb22:s htr11:p hex10:v htr21:p
-gb20:s mx132:p hex11:v ln30:s htr22:p hex21:v ln32:s htr20:p hex22:v btr61:p gb32:s hex20:v mx133:p
-gb30:s hq1:v mx131:p ln33:s hq2:v htr32:p bev61:s htr30:p gb33:v mx23_0:p hex32:v ln31:s gb31:v
-htr33:p hex30:v oev3_0:s htr31:p hex33:v mx22_0:p hex31:v mx21_0:p bq4:v oev2_0:s hq3:v mx20_0:p
-oev1_0:s bq6:v mx22_1:p oev0_0:s mx24_0:p oev2_1:v bq7:v mx21_1:p mx25_0:p oev4_0:v oev1_1:v
-mx23_1:p oev5_0:v mx26_0:p oev3_1:v mx20_1:p oev6_0:v mx27_0:p oev0_1:v oev7_0:v
+dum9:p dum20:p st0:p rowsf:v st1:p sev0:v dum19:p sev1:s fil11:s prod11:v fil10:s prod10:v prod12:v
+fil01:s ptr101:p prod13:v dum21:p fil00:s dum13:p prod22:v ptr111:p pev101:s prod01:v ptr110:p
+pev111:s dum4:p pev110:s dum15:p ptr100:p prod23:v btr11:p pev100:s dum17:p prod00:v bev11:s btr71:p
+dum16:p bev71:s ptr210:p pq11:v btr10:p pq10:v pev210:s ptr000:p bev10:s fq1:v dum7:p pt:p pev000:s
+dum3:p fq0:v ptr001:p cols:v prod03:v btr31:p pev001:s mx113:p bev31:s prod02:v btr61:p ln13:s
+btr20:p bev61:s bq1:v btr30:p bev20:s prod21:v ptr011:p bev30:s mx112:p pev011:s prod30:v mx110:p
+ln12:s ptr010:p gb13:s prod20:v btr40:p pev010:s mx111:p ln10:s pq00:v htr13:p bev40:s pq01:v
+ptr200:p ln11:s btr70:p hex13:v gb12:s mx101:p prod32:v pev200:s mx102:p bev70:s prod31:v ptr201:p
+ln01:s ptr211:p pev201:s prod33:v htr12:p gb11:s mx103:p pev211:s hex12:v ptr301:p ln02:s pq21:v
+htr11:p ptr310:p ln03:s pq20:v mx100:p pev301:s gb10:v gb01:v pev310:s mx120:p hex11:v ptr311:p
+ln00:s bq7:v gb03:s htr10:p pev311:v btr01:p gb00:s gb02:v mx122:p ln20:s hex10:v ptr300:p bev01:s
+bq3:v htr01:p pq31:v pev300:s htr03:p mx121:p hex01:v gb20:s htr02:p hex03:v ln22:s btr21:p ln21:s
+hex02:v btr60:p bev21:s pq30:v htr00:p bev60:s mx123:p gb21:v hq1:v gb22:s mx132:p hex00:v ln23:s
+htr20:p bq6:v htr22:p ln32:s btr51:p hex20:v gb23:s mx130:p hex22:v bev51:s htr23:p gb32:v ln30:s
+bq2:v htr21:p btr00:p gb30:s hq0:v mx131:p bev00:s hex23:v mx133:p hex21:v ln31:s htr30:p ln33:s
+hq2:v btr50:p htr32:p hex30:v bev50:s mx26_0:p gb31:v gb33:s hex32:v mx27_0:p oev6_0:s bq0:v btr41:p
+bq5:v oev7_0:v htr31:p htr33:p hex31:v mx25_0:p hex33:v mx20_0:p bev41:v hq3:v mx23_0:p oev5_0:v
+mx20_1:p bq4:v mx25_1:p mx22_0:p oev0_0:v oev5_1:v mx23_1:p mx27_1:p mx22_1:p oev3_0:v mx24_0:p
+oev2_0:v mx24_1:p oev7_1:v mx26_1:p mx21_0:p oev4_0:v oev6_1:v mx21_1:p oev1_0:v
 """
 
 P = 128
-SPLIT = [[[0, 1, 2], [3]]] * 4 + [[[0, 1, 2, 3]]] * 4
 GROUPS = T // 512
 PASSES = K // 512
 FB = F // P
@@ -66,6 +68,7 @@ def tile_temporal_log_mel_cepstrum_f4_kernel(
         rows_f = const.tile([P, P], F32, name="rows_f")
         cols = const.tile([P, 20], F32, name="cols")
         fw = const.tile([P, GROUPS, 4], BF16, name="fw")
+        warm_bf = const.tile([P, 512], BF16, name="warm_bf")
 
         code_in = [keep.tile([P, 4, K], U8, name="code_in%d" % g) for g in range(GROUPS)]
         f_raw = [keep.tile([P, 4, F], BF16, name="f_raw%d" % s) for s in range(PASSES)]
@@ -88,6 +91,7 @@ def tile_temporal_log_mel_cepstrum_f4_kernel(
         nc.vector.memset(rows_bf[:], 0.0)
         nc.vector.memset(warm[:], 1.0)
         make_identity(nc, ident[:])
+        nc.gpsimd.memset(warm_bf[:], 0.0)
         nc.scalar.activation(out=warm_out[:], in_=warm[:], func=ACT.Ln)
 
         load(s_col[:], power_scale.rearrange("o (p j) -> p (o j)", p=P))
@@ -95,25 +99,25 @@ def tile_temporal_log_mel_cepstrum_f4_kernel(
         load(rows_bf[4:8, :], gain.rearrange("(c p) -> c p", p=P))
         load(rows_bf[8:12, :], bias.rearrange("(c p) -> c p", p=P))
         load(rows_bf[12:20, :], lifter.rearrange("(c p) -> c p", p=P))
-        load(b_raw[5][:], b_src[5])
-        load(code_in[0][:, 2:4, :], p_src[0][:, 2:4, :])
-        load(f_raw[0][:], f_src[0])
-        load(code_in[0][:, 0:2, :], p_src[0][:, 0:2, :])
+        load(fw[:], frame_weight.rearrange("(g p t) -> p g t", p=P, t=4))
+        load(code_in[1][:, 0:2, :], p_src[1][:, 0:2, :])
         load(f_raw[1][:], f_src[1])
         load(code_in[1][:, 2:4, :], p_src[1][:, 2:4, :])
+        load(f_raw[0][:], f_src[0])
+        load(b_raw[7][:], b_src[7])
         load(code_in[2][:, 2:4, :], p_src[2][:, 2:4, :])
-        load(code_in[1][:, 0:2, :], p_src[1][:, 0:2, :])
-        load(fw[:], frame_weight.rearrange("(g p t) -> p g t", p=P, t=4))
+        load(code_in[0][:, 2:4, :], p_src[0][:, 2:4, :])
+        load(code_in[3][:, 0:2, :], p_src[3][:, 0:2, :])
+        load(code_in[0][:, 0:2, :], p_src[0][:, 0:2, :])
         load(b_raw[1][:], b_src[1])
-        load(b_raw[4][:], b_src[4])
+        load(b_raw[2][:], b_src[2])
+        load(b_raw[6][:], b_src[6])
+        load(b_raw[5][:], b_src[5])
         load(b_raw[3][:], b_src[3])
         load(code_in[2][:, 0:2, :], p_src[2][:, 0:2, :])
-        load(b_raw[2][:], b_src[2])
         load(b_raw[0][:], b_src[0])
+        load(b_raw[4][:], b_src[4])
         load(code_in[3][:, 2:4, :], p_src[3][:, 2:4, :])
-        load(code_in[3][:, 0:2, :], p_src[3][:, 0:2, :])
-        load(b_raw[6][:], b_src[6])
-        load(b_raw[7][:], b_src[7])
 
         x_tiles, p_tr, p_il, p_codes, p_scales = {}, {}, {}, {}, {}
         b_tr, b_il = {}, {}
@@ -121,10 +125,17 @@ def tile_temporal_log_mel_cepstrum_f4_kernel(
         c_acc = {}
 
         st_t = {}
+        pending = []
+
+        def warmups(tile_2d):
+            for x in pending:
+                nc.tensor.matmul(tile_2d, lhsT=warm_bf[:, 0:P], rhs=warm_bf[:], start=True, stop=True)
+            pending.clear()
 
         def scale_tr(half):
             st = tr_pool.tile([P, 4, P], F32, name="st", tag="tr")
             st_t[half] = st
+            warmups(st[:].rearrange("p j n -> p (j n)"))
             for j in range(4):
                 jj = 4 * half + j
                 nc.tensor.transpose(st[:, j, :], s_col[:, jj : jj + 1].to_broadcast([P, P]), ident[:])
@@ -171,6 +182,7 @@ def tile_temporal_log_mel_cepstrum_f4_kernel(
         def ptr(g, tp, s):
             pt = tr_pool.tile([P, 2, 2, P], F32, name="p_tr", tag="tr")
             p_tr[g, tp, s] = pt
+            warmups(pt[:].rearrange("p u t r -> p (u t r)"))
             words = x_tiles[g][:].rearrange("p t k -> p (t k)").bitcast(F32)
             for u in range(2):
                 for tt in range(2):
@@ -219,6 +231,7 @@ def tile_temporal_log_mel_cepstrum_f4_kernel(
         def htr(g, fb):
             ht = tr_pool.tile([P, 4, P], F32, name="h_tr", tag="tr")
             h_tr[g, fb] = ht
+            warmups(ht[:].rearrange("p t f -> p (t f)"))
             for t in range(4):
                 nc.tensor.transpose(ht[:, t, :], y_tiles[g, fb][:, P * t : P * (t + 1)], ident[:])
 
@@ -237,6 +250,7 @@ def tile_temporal_log_mel_cepstrum_f4_kernel(
         def btr(q, h):
             bt = tr_pool.tile([P, 2, 2, P], F32, name="b_tr", tag="tr")
             b_tr[q, h] = bt
+            warmups(bt[:].rearrange("p g u q -> p (g u q)"))
             words = b_raw[q][:].bitcast(F32)
             for gg in range(2):
                 for u in range(2):
@@ -257,19 +271,36 @@ def tile_temporal_log_mel_cepstrum_f4_kernel(
 
         parts = {}
 
-        def mx2(q, i):
-            c = c_pool.tile([P, F], F32, name="c_acc", tag="c")
-            c_acc[q, i] = c
-            gs = SPLIT[q][i]
+        def c_tile(kind):
+            if kind == "e":
+                c = e_pool.tile([P, F], F32, name="c_acc_e", tag="e")
+            elif kind == "t":
+                c = tr_pool.tile([P, F], F32, name="c_acc_t", tag="tr")
+            else:
+                c = c_pool.tile([P, F], F32, name="c_acc", tag="c")
+            return c
+
+        def passes(c, q, gs, first, last):
             for g in gs:
                 cs = slice(P * g, P * (g + 1))
                 nc.tensor.matmul_mx(
                     out=c[:], lhsT=b_codes[q][:, cs].bitcast(FP8X4), lhsT_scale=b_scales[q][:, cs],
                     rhs=h_codes[g][:].bitcast(FP8X4), rhs_scale=h_scales[g][:],
-                    start=(g == gs[0]), stop=(g == gs[-1]))
+                    start=(g == first), stop=(g == last))
+
+        def mx2(q, i):
+            kind = PLAN[q]
+            if kind in "cet":
+                if i == 0:
+                    c_acc[q, 0] = c_tile(kind)
+                passes(c_acc[q, 0], q, [[0, 1, 2], [3]][i], 0, 3)
+            else:
+                gs = {"p": [[0, 1, 2], [3]], "h": [[0, 1], [2, 3]], "f": [[0, 1, 2, 3]]}[kind][i]
+                c_acc[q, i] = c_tile("c")
+                passes(c_acc[q, i], q, gs, gs[0], gs[-1])
 
         def oev(q, i, eng):
-            last = i == len(SPLIT[q]) - 1
+            last = i == 1 or PLAN[q] not in "ph"
             o = work.tile([P, F], F32, name="o_t", tag="o_t" if last else "part_t", bufs=4)
             sc = cols[:, 12 + q : 13 + q]
             src = c_acc[q, i]
@@ -284,7 +315,10 @@ def tile_temporal_log_mel_cepstrum_f4_kernel(
                 nc.sync.dma_start(out=out[P * q : P * (q + 1), :], in_=o[:])
 
         def run_step(name, eng):
-            if name.startswith("st"):
+            if name.startswith("dum"):
+                if eng == "p":
+                    pending.append(name)
+            elif name.startswith("st"):
                 scale_tr(int(name[2:]))
             elif name.startswith("sev"):
                 scale_ev(int(name[3:]), eng)

@@ -6,28 +6,27 @@ from concourse.masks import make_identity
 T, K, F, Q = 2048, 1024, 512, 1024
 FLOPS = 2 * T * K * F + 2 * Q * T * F
 
-PLAN = "ccceeppp"
+PLAN = "ccceettt"
 
 STEPS = """
-dum9:p dum20:p st0:p rowsf:v st1:p sev0:v dum19:p sev1:s fil11:s prod11:v fil10:s prod10:v prod12:v
-fil01:s ptr101:p prod13:v dum21:p fil00:s dum13:p prod22:v ptr111:p pev101:s prod01:v ptr110:p
-pev111:s dum4:p pev110:s dum15:p ptr100:p prod23:v btr11:p pev100:s dum17:p prod00:v bev11:s btr71:p
-dum16:p bev71:s ptr210:p pq11:v btr10:p pq10:v pev210:s ptr000:p bev10:s fq1:v dum7:p pt:p pev000:s
-dum3:p fq0:v ptr001:p cols:v prod03:v btr31:p pev001:s mx113:p bev31:s prod02:v btr61:p ln13:s
-btr20:p bev61:s bq1:v btr30:p bev20:s prod21:v ptr011:p bev30:s mx112:p pev011:s prod30:v mx110:p
-ln12:s ptr010:p gb13:s prod20:v btr40:p pev010:s mx111:p ln10:s pq00:v htr13:p bev40:s pq01:v
-ptr200:p ln11:s btr70:p hex13:v gb12:s mx101:p prod32:v pev200:s mx102:p bev70:s prod31:v ptr201:p
-ln01:s ptr211:p pev201:s prod33:v htr12:p gb11:s mx103:p pev211:s hex12:v ptr301:p ln02:s pq21:v
-htr11:p ptr310:p ln03:s pq20:v mx100:p pev301:s gb10:v gb01:v pev310:s mx120:p hex11:v ptr311:p
-ln00:s bq7:v gb03:s htr10:p pev311:v btr01:p gb00:s gb02:v mx122:p ln20:s hex10:v ptr300:p bev01:s
-bq3:v htr01:p pq31:v pev300:s htr03:p mx121:p hex01:v gb20:s htr02:p hex03:v ln22:s btr21:p ln21:s
-hex02:v btr60:p bev21:s pq30:v htr00:p bev60:s mx123:p gb21:v hq1:v gb22:s mx132:p hex00:v ln23:s
-htr20:p bq6:v htr22:p ln32:s btr51:p hex20:v gb23:s mx130:p hex22:v bev51:s htr23:p gb32:v ln30:s
-bq2:v htr21:p btr00:p gb30:s hq0:v mx131:p bev00:s hex23:v mx133:p hex21:v ln31:s htr30:p ln33:s
-hq2:v btr50:p htr32:p hex30:v bev50:s mx26_0:p gb31:v gb33:s hex32:v mx27_0:p oev6_0:s bq0:v btr41:p
-bq5:v oev7_0:v htr31:p htr33:p hex31:v mx25_0:p hex33:v mx20_0:p bev41:v hq3:v mx23_0:p oev5_0:v
-mx20_1:p bq4:v mx25_1:p mx22_0:p oev0_0:v oev5_1:v mx23_1:p mx27_1:p mx22_1:p oev3_0:v mx24_0:p
-oev2_0:v mx24_1:p oev7_1:v mx26_1:p mx21_0:p oev4_0:v oev6_1:v mx21_1:p oev1_0:v
+rowsf:v st0:p st1:p sev0:s pt:p sev1:v cols:v prod10:v fil01:s fil00:s prod01:v prod11:v fil11:s
+btr40:p fil10:s prod12:v ptr100:p bev40:s pev100:s prod13:v btr20:p bev20:s ptr101:p btr21:p
+prod00:v pev101:s ptr111:p ptr001:p bev21:s pev111:s prod02:v prod03:v ptr000:p pev001:s ptr110:p
+pev000:s fq0:v btr60:p pev110:s btr41:p pq11:v bev60:s pq10:v ptr011:p btr51:p bev41:s pev011:s
+fq1:v ptr010:p prod22:v bev51:s prod23:v btr50:p pev010:s mx111:p bev50:s ln11:s mx113:p ln13:s
+btr00:p bev00:s gb11:s mx112:p pq01:v ptr210:p pev210:s ptr211:p ln12:s pq00:v btr61:p bev61:s
+prod30:v pev211:s mx110:p ln10:s mx102:p ln02:s prod31:v prod20:v htr11:p prod21:v hex11:v prod32:v
+ptr301:p pev301:s btr01:p bev01:s mx101:p ln01:s gb01:s mx100:p ptr300:p ptr200:p pev300:s prod33:v
+htr01:p pev200:s gb13:v gb12:s ptr201:p hex01:v ptr310:p gb10:v mx103:p pev201:s pev310:s pq20:v
+htr12:p ln00:s ln03:s pq21:v ptr311:p btr30:p mx120:p pev311:s hex12:v gb02:s gb00:v mx121:p ln20:s
+bq4:v htr13:p htr02:p bev30:s pq30:v hex13:v mx123:p ln21:s hex02:v ln23:s gb23:s htr00:p htr10:p
+btr31:p mx122:p pq31:v hex00:v gb03:s mx133:p bev31:s hex10:v gb20:v ln22:s htr03:p bq2:v gb21:s
+btr11:p bev11:s htr23:p mx132:p hex03:v hq1:v hex23:v ln33:s htr20:p hex20:v gb22:s htr21:p hex21:v
+ln32:s gb32:s mx131:p htr22:p hex22:v btr10:p bev10:s btr70:p ln31:s gb31:s gb33:s btr71:p hq0:v
+hq2:v htr32:p mx130:p ln30:s bq0:v mx22_0:p mx20_0:p bq6:v bev70:s bq1:v mx24_0:p bq3:v htr31:p
+bev71:s htr33:p gb30:s hex32:v hex31:v htr30:p hex30:v mx23_0:p mx21_0:p mx26_0:p hex33:v hq3:v
+mx22_1:p mx23_1:p oev2_0:s bq5:v bq7:v oev3_0:v mx21_1:p oev1_0:s mx24_1:p oev4_0:s mx26_1:p
+oev6_0:s mx20_1:p oev0_0:s mx27_0:p mx27_1:p oev7_0:s mx25_0:p mx25_1:p oev5_0:s
 """
 
 P = 128
@@ -99,25 +98,25 @@ def tile_temporal_log_mel_cepstrum_f4_kernel(
         load(rows_bf[4:8, :], gain.rearrange("(c p) -> c p", p=P))
         load(rows_bf[8:12, :], bias.rearrange("(c p) -> c p", p=P))
         load(rows_bf[12:20, :], lifter.rearrange("(c p) -> c p", p=P))
-        load(fw[:], frame_weight.rearrange("(g p t) -> p g t", p=P, t=4))
-        load(code_in[1][:, 0:2, :], p_src[1][:, 0:2, :])
-        load(f_raw[1][:], f_src[1])
-        load(code_in[1][:, 2:4, :], p_src[1][:, 2:4, :])
         load(f_raw[0][:], f_src[0])
-        load(b_raw[7][:], b_src[7])
-        load(code_in[2][:, 2:4, :], p_src[2][:, 2:4, :])
-        load(code_in[0][:, 2:4, :], p_src[0][:, 2:4, :])
-        load(code_in[3][:, 0:2, :], p_src[3][:, 0:2, :])
+        load(code_in[1][:, 0:2, :], p_src[1][:, 0:2, :])
         load(code_in[0][:, 0:2, :], p_src[0][:, 0:2, :])
-        load(b_raw[1][:], b_src[1])
+        load(f_raw[1][:], f_src[1])
+        load(b_raw[4][:], b_src[4])
+        load(code_in[1][:, 2:4, :], p_src[1][:, 2:4, :])
         load(b_raw[2][:], b_src[2])
+        load(code_in[2][:, 2:4, :], p_src[2][:, 2:4, :])
+        load(fw[:], frame_weight.rearrange("(g p t) -> p g t", p=P, t=4))
+        load(b_raw[1][:], b_src[1])
+        load(code_in[0][:, 2:4, :], p_src[0][:, 2:4, :])
         load(b_raw[6][:], b_src[6])
+        load(code_in[3][:, 0:2, :], p_src[3][:, 0:2, :])
+        load(code_in[3][:, 2:4, :], p_src[3][:, 2:4, :])
         load(b_raw[5][:], b_src[5])
-        load(b_raw[3][:], b_src[3])
+        load(b_raw[7][:], b_src[7])
         load(code_in[2][:, 0:2, :], p_src[2][:, 0:2, :])
         load(b_raw[0][:], b_src[0])
-        load(b_raw[4][:], b_src[4])
-        load(code_in[3][:, 2:4, :], p_src[3][:, 2:4, :])
+        load(b_raw[3][:], b_src[3])
 
         x_tiles, p_tr, p_il, p_codes, p_scales = {}, {}, {}, {}, {}
         b_tr, b_il = {}, {}

from contextlib import ExitStack

import concourse.mybir as mybir
from concourse.masks import make_identity

T, K, F, Q = 2048, 1024, 512, 1024
FLOPS = 2 * T * K * F + 2 * Q * T * F

PLAN = "ccceettt"

STEPS = """
rowsf:v st0:p st1:p sev0:s pt:p sev1:v cols:v prod10:v fil01:s fil00:s prod01:v prod11:v fil11:s
btr40:p fil10:s prod12:v ptr100:p bev40:s pev100:s prod13:v btr20:p bev20:s ptr101:p btr21:p
prod00:v pev101:s ptr111:p ptr001:p bev21:s pev111:s prod02:v prod03:v ptr000:p pev001:s ptr110:p
pev000:s fq0:v btr60:p pev110:s btr41:p pq11:v bev60:s pq10:v ptr011:p btr51:p bev41:s pev011:s
fq1:v ptr010:p prod22:v bev51:s prod23:v btr50:p pev010:s mx111:p bev50:s ln11:s mx113:p ln13:s
btr00:p bev00:s gb11:s mx112:p pq01:v ptr210:p pev210:s ptr211:p ln12:s pq00:v btr61:p bev61:s
prod30:v pev211:s mx110:p ln10:s mx102:p ln02:s prod31:v prod20:v htr11:p prod21:v hex11:v prod32:v
ptr301:p pev301:s btr01:p bev01:s mx101:p ln01:s gb01:s mx100:p ptr300:p ptr200:p pev300:s prod33:v
htr01:p pev200:s gb13:v gb12:s ptr201:p hex01:v ptr310:p gb10:v mx103:p pev201:s pev310:s pq20:v
htr12:p ln00:s ln03:s pq21:v ptr311:p btr30:p mx120:p pev311:s hex12:v gb02:s gb00:v mx121:p ln20:s
bq4:v htr13:p htr02:p bev30:s pq30:v hex13:v mx123:p ln21:s hex02:v ln23:s gb23:s htr00:p htr10:p
btr31:p mx122:p pq31:v hex00:v gb03:s mx133:p bev31:s hex10:v gb20:v ln22:s htr03:p bq2:v gb21:s
btr11:p bev11:s htr23:p mx132:p hex03:v hq1:v hex23:v ln33:s htr20:p hex20:v gb22:s htr21:p hex21:v
ln32:s gb32:s mx131:p htr22:p hex22:v btr10:p bev10:s btr70:p ln31:s gb31:s gb33:s btr71:p hq0:v
hq2:v htr32:p mx130:p ln30:s bq0:v mx22_0:p mx20_0:p bq6:v bev70:s bq1:v mx24_0:p bq3:v htr31:p
bev71:s htr33:p gb30:s hex32:v hex31:v htr30:p hex30:v mx23_0:p mx21_0:p mx26_0:p hex33:v hq3:v
mx22_1:p mx23_1:p oev2_0:s bq5:v bq7:v oev3_0:v mx21_1:p oev1_0:s mx24_1:p oev4_0:s mx26_1:p
oev6_0:s mx20_1:p oev0_0:s mx27_0:p mx27_1:p oev7_0:s mx25_0:p mx25_1:p oev5_0:s
"""

P = 128
GROUPS = T // 512
PASSES = K // 512
FB = F // P
QT = Q // P

F32 = mybir.dt.float32
BF16 = mybir.dt.bfloat16
U32 = mybir.dt.uint32
U8 = mybir.dt.uint8
FP8 = mybir.dt.float8_e4m3fn
FP8X4 = mybir.dt.float8_e4m3fn_x4
ALU = mybir.AluOpType
ACT = mybir.ActivationFunctionType


def tile_temporal_log_mel_cepstrum_f4_kernel(
    tc, power_bytes, power_scale, filters, offset, gain, bias, frame_weight, basis, lifter, out
):
    nc = tc.nc
    with ExitStack() as ctx:
        const = ctx.enter_context(tc.tile_pool(name="const", bufs=1))
        keep = ctx.enter_context(tc.tile_pool(name="keep", bufs=1))
        work = ctx.enter_context(tc.tile_pool(name="work", bufs=2))
        tr_pool = ctx.enter_context(tc.psum_pool(name="tr", bufs=3))
        e_pool = ctx.enter_context(tc.psum_pool(name="epool", bufs=2))
        c_pool = ctx.enter_context(tc.psum_pool(name="cpool", bufs=3))
        ctx.enter_context(tc.manual_schedule())

        ident = const.tile([P, P], F32, name="ident")
        warm = const.tile([P, 1], F32, name="warm")
        warm_out = const.tile([P, 1], F32, name="warm_out")
        s_col = const.tile([P, 8], F32, name="s_col")
        s_row = const.tile([P, K], F32, name="s_row")
        rows_bf = const.tile([P, P], BF16, name="rows_bf")
        rows_f = const.tile([P, P], F32, name="rows_f")
        cols = const.tile([P, 20], F32, name="cols")
        fw = const.tile([P, GROUPS, 4], BF16, name="fw")
        warm_bf = const.tile([P, 512], BF16, name="warm_bf")

        code_in = [keep.tile([P, 4, K], U8, name="code_in%d" % g) for g in range(GROUPS)]
        f_raw = [keep.tile([P, 4, F], BF16, name="f_raw%d" % s) for s in range(PASSES)]
        f_il = [keep.tile([P, F, 4], BF16, name="f_il%d" % s, align_bytes=64) for s in range(PASSES)]
        f_codes = [keep.tile([P, F], U32, name="f_codes%d" % s, align_bytes=64) for s in range(PASSES)]
        f_scales = [keep.tile([P, F], U8, name="f_scales%d" % s, align_bytes=64) for s in range(PASSES)]
        b_raw = [keep.tile([P, T], BF16, name="b_raw%d" % q) for q in range(QT)]
        b_codes = [keep.tile([P, 512], U32, name="b_codes%d" % q, align_bytes=64) for q in range(QT)]
        b_scales = [keep.tile([P, 512], U8, name="b_scales%d" % q, align_bytes=64) for q in range(QT)]
        h_codes = [keep.tile([P, F], U32, name="h_codes%d" % g, align_bytes=64) for g in range(GROUPS)]
        h_scales = [keep.tile([P, F], U8, name="h_scales%d" % g, align_bytes=64) for g in range(GROUPS)]

        p_src = power_bytes.rearrange("(g p t) k -> g p t k", p=P, t=4)
        f_src = filters.rearrange("(s p j) w -> s p j w", p=P, j=4)
        b_src = basis.rearrange("(q p) t -> q p t", p=P)

        def load(dst, src):
            nc.sync.dma_start(out=dst, in_=src)

        nc.vector.memset(rows_bf[:], 0.0)
        nc.vector.memset(warm[:], 1.0)
        make_identity(nc, ident[:])
        nc.gpsimd.memset(warm_bf[:], 0.0)
        nc.scalar.activation(out=warm_out[:], in_=warm[:], func=ACT.Ln)

        load(s_col[:], power_scale.rearrange("o (p j) -> p (o j)", p=P))
        load(rows_bf[0:4, :], offset.rearrange("(c p) -> c p", p=P))
        load(rows_bf[4:8, :], gain.rearrange("(c p) -> c p", p=P))
        load(rows_bf[8:12, :], bias.rearrange("(c p) -> c p", p=P))
        load(rows_bf[12:20, :], lifter.rearrange("(c p) -> c p", p=P))
        load(f_raw[0][:], f_src[0])
        load(code_in[1][:, 0:2, :], p_src[1][:, 0:2, :])
        load(code_in[0][:, 0:2, :], p_src[0][:, 0:2, :])
        load(f_raw[1][:], f_src[1])
        load(b_raw[4][:], b_src[4])
        load(code_in[1][:, 2:4, :], p_src[1][:, 2:4, :])
        load(b_raw[2][:], b_src[2])
        load(code_in[2][:, 2:4, :], p_src[2][:, 2:4, :])
        load(fw[:], frame_weight.rearrange("(g p t) -> p g t", p=P, t=4))
        load(b_raw[1][:], b_src[1])
        load(code_in[0][:, 2:4, :], p_src[0][:, 2:4, :])
        load(b_raw[6][:], b_src[6])
        load(code_in[3][:, 0:2, :], p_src[3][:, 0:2, :])
        load(code_in[3][:, 2:4, :], p_src[3][:, 2:4, :])
        load(b_raw[5][:], b_src[5])
        load(b_raw[7][:], b_src[7])
        load(code_in[2][:, 0:2, :], p_src[2][:, 0:2, :])
        load(b_raw[0][:], b_src[0])
        load(b_raw[3][:], b_src[3])

        x_tiles, p_tr, p_il, p_codes, p_scales = {}, {}, {}, {}, {}
        b_tr, b_il = {}, {}
        e_acc, l_tiles, y_tiles, h_tr, h_il = {}, {}, {}, {}, {}
        c_acc = {}

        st_t = {}
        pending = []

        def warmups(tile_2d):
            for x in pending:
                nc.tensor.matmul(tile_2d, lhsT=warm_bf[:, 0:P], rhs=warm_bf[:], start=True, stop=True)
            pending.clear()

        def scale_tr(half):
            st = tr_pool.tile([P, 4, P], F32, name="st", tag="tr")
            st_t[half] = st
            warmups(st[:].rearrange("p j n -> p (j n)"))
            for j in range(4):
                jj = 4 * half + j
                nc.tensor.transpose(st[:, j, :], s_col[:, jj : jj + 1].to_broadcast([P, P]), ident[:])

        def copy(eng, dst, src):
            if eng == "v":
                nc.vector.tensor_copy(out=dst, in_=src)
            else:
                nc.scalar.copy(out=dst, in_=src)

        def scale_ev(half, eng):
            dst = s_row[:].rearrange("p (n j) -> p n j", j=8)[:, :, 4 * half : 4 * half + 4]
            copy(eng, dst, st_t[half][:].rearrange("p j n -> p n j"))

        def par(step):
            if step == 0:
                nc.vector.tensor_copy(out=rows_f[:], in_=rows_bf[:])
            elif step == 1:
                pt = tr_pool.tile([P, P], F32, name="pt", tag="tr")
                st_t["pt"] = pt
                nc.tensor.transpose(pt[:], rows_f[:], ident[:])
            else:
                nc.vector.tensor_copy(out=cols[:], in_=st_t["pt"][:, 0:20])

        def f_interleave(s, eng, lo, hi):
            src = f_raw[s][:, :, lo:hi].rearrange("p j w -> p w j")
            if eng == "v":
                nc.vector.tensor_copy(out=f_il[s][:, lo:hi, :], in_=src)
            else:
                nc.scalar.copy(out=f_il[s][:, lo:hi, :], in_=src)

        def f_quant(s):
            nc.vector.quantize_mx(
                out=f_codes[s][:].bitcast(FP8X4), scales=f_scales[s][:],
                in_=f_il[s][:].rearrange("p w j -> p (w j)"))

        def prod(g, t):
            if g not in x_tiles:
                x = work.tile([P, 4, K], BF16, name="x_bf", tag="x_bf", bufs=4)
                x_tiles[g] = x
            nc.vector.tensor_tensor(
                out=x_tiles[g][:, t, :], in0=code_in[g][:, t, :].bitcast(FP8), in1=s_row[:], op=ALU.mult)

        def ptr(g, tp, s):
            pt = tr_pool.tile([P, 2, 2, P], F32, name="p_tr", tag="tr")
            p_tr[g, tp, s] = pt
            warmups(pt[:].rearrange("p u t r -> p (u t r)"))
            words = x_tiles[g][:].rearrange("p t k -> p (t k)").bitcast(F32)
            for u in range(2):
                for tt in range(2):
                    base = 512 * (2 * tp + tt) + 256 * s
                    nc.tensor.transpose(pt[:, u, tt, :], words[:, base + u : base + 256 : 2], ident[:])

        def pev(g, tp, s, eng):
            if (g, s) not in p_il:
                il = work.tile([P, 512, 4], BF16, name="p_il", tag="p_il", bufs=5, align_bytes=64)
                p_il[g, s] = il
            words = p_il[g, s][:].rearrange("p n j -> p (n j)").bitcast(F32)
            dst = words[:, 512 * tp : 512 * (tp + 1)].rearrange("p (n u) -> p n u", u=2)
            copy(eng, dst, p_tr[g, tp, s][:].rearrange("p u t r -> p (t r) u"))

        def pq(g, s):
            codes = work.tile([P, 512], U32, name="p_codes", tag="p_codes", bufs=5, align_bytes=64)
            scales = work.tile([P, 512], U8, name="p_scales", tag="p_scales", bufs=5, align_bytes=64)
            p_codes[g, s], p_scales[g, s] = codes, scales
            nc.vector.quantize_mx(out=codes[:].bitcast(FP8X4), scales=scales[:],
                                  in_=p_il[g, s][:].rearrange("p n j -> p (n j)"))

        def mx1(g, fb):
            e = e_pool.tile([P, 512], F32, name="e_acc", tag="e")
            e_acc[g, fb] = e
            c = slice(P * fb, P * (fb + 1))
            for s in range(PASSES):
                nc.tensor.matmul_mx(
                    out=e[:], lhsT=f_codes[s][:, c].bitcast(FP8X4), lhsT_scale=f_scales[s][:, c],
                    rhs=p_codes[g, s][:].bitcast(FP8X4), rhs_scale=p_scales[g, s][:],
                    start=(s == 0), stop=(s == PASSES - 1))

        def ln(g, fb):
            l = work.tile([P, 512], F32, name="l_t", tag="l_t", bufs=5)
            l_tiles[g, fb] = l
            nc.scalar.activation(out=l[:], in_=e_acc[g, fb][:], func=ACT.Ln, bias=cols[:, fb : fb + 1], scale=1.0)

        def gb(g, fb, eng):
            y = work.tile([P, 512], F32, name="y_t", tag="y_t", bufs=5)
            y_tiles[g, fb] = y
            gc, bc = cols[:, 4 + fb : 5 + fb], cols[:, 8 + fb : 9 + fb]
            if eng == "v":
                nc.vector.tensor_scalar(out=y[:], in0=l_tiles[g, fb][:], scalar1=gc, scalar2=bc, op0=ALU.mult, op1=ALU.add)
            else:
                nc.scalar.activation(out=y[:], in_=l_tiles[g, fb][:], func=ACT.Identity, bias=bc, scale=gc)

        def htr(g, fb):
            ht = tr_pool.tile([P, 4, P], F32, name="h_tr", tag="tr")
            h_tr[g, fb] = ht
            warmups(ht[:].rearrange("p t f -> p (t f)"))
            for t in range(4):
                nc.tensor.transpose(ht[:, t, :], y_tiles[g, fb][:, P * t : P * (t + 1)], ident[:])

        def hex_(g, fb):
            if g not in h_il:
                il = work.tile([P, F, 4], BF16, name="h_il", tag="h_il", bufs=2, align_bytes=64)
                h_il[g] = il
            nc.vector.tensor_tensor(
                out=h_il[g][:, P * fb : P * (fb + 1), :], in0=h_tr[g, fb][:].rearrange("p t f -> p f t"),
                in1=fw[:, g, :].unsqueeze(1).to_broadcast([P, P, 4]), op=ALU.mult)

        def hq(g):
            nc.vector.quantize_mx(out=h_codes[g][:].bitcast(FP8X4), scales=h_scales[g][:],
                                  in_=h_il[g][:].rearrange("p f t -> p (f t)"))

        def btr(q, h):
            bt = tr_pool.tile([P, 2, 2, P], F32, name="b_tr", tag="tr")
            b_tr[q, h] = bt
            warmups(bt[:].rearrange("p g u q -> p (g u q)"))
            words = b_raw[q][:].bitcast(F32)
            for gg in range(2):
                for u in range(2):
                    base = 256 * (2 * h + gg)
                    nc.tensor.transpose(bt[:, gg, u, :], words[:, base + u : base + 256 : 2], ident[:])

        def bev(q, h, eng):
            if q not in b_il:
                il = work.tile([P, 4, P, 4], BF16, name="b_il", tag="b_il", bufs=5, align_bytes=64)
                b_il[q] = il
            words = b_il[q][:].rearrange("p g q j -> p (g q j)").bitcast(F32)
            dst = words[:, 512 * h : 512 * (h + 1)].rearrange("p (g q u) -> p g q u", g=2, u=2)
            copy(eng, dst, b_tr[q, h][:].rearrange("p g u q -> p g q u"))

        def bq(q):
            nc.vector.quantize_mx(out=b_codes[q][:].bitcast(FP8X4), scales=b_scales[q][:],
                                  in_=b_il[q][:].rearrange("p g q j -> p (g q j)"))

        parts = {}

        def c_tile(kind):
            if kind == "e":
                c = e_pool.tile([P, F], F32, name="c_acc_e", tag="e")
            elif kind == "t":
                c = tr_pool.tile([P, F], F32, name="c_acc_t", tag="tr")
            else:
                c = c_pool.tile([P, F], F32, name="c_acc", tag="c")
            return c

        def passes(c, q, gs, first, last):
            for g in gs:
                cs = slice(P * g, P * (g + 1))
                nc.tensor.matmul_mx(
                    out=c[:], lhsT=b_codes[q][:, cs].bitcast(FP8X4), lhsT_scale=b_scales[q][:, cs],
                    rhs=h_codes[g][:].bitcast(FP8X4), rhs_scale=h_scales[g][:],
                    start=(g == first), stop=(g == last))

        def mx2(q, i):
            kind = PLAN[q]
            if kind in "cet":
                if i == 0:
                    c_acc[q, 0] = c_tile(kind)
                passes(c_acc[q, 0], q, [[0, 1, 2], [3]][i], 0, 3)
            else:
                gs = {"p": [[0, 1, 2], [3]], "h": [[0, 1], [2, 3]], "f": [[0, 1, 2, 3]]}[kind][i]
                c_acc[q, i] = c_tile("c")
                passes(c_acc[q, i], q, gs, gs[0], gs[-1])

        def oev(q, i, eng):
            last = i == 1 or PLAN[q] not in "ph"
            o = work.tile([P, F], F32, name="o_t", tag="o_t" if last else "part_t", bufs=4)
            sc = cols[:, 12 + q : 13 + q]
            src = c_acc[q, i]
            if i > 0:
                nc.vector.scalar_tensor_tensor(out=o[:], in0=src[:], scalar=sc, in1=parts[q][:], op0=ALU.mult, op1=ALU.add)
            elif eng == "v":
                nc.vector.tensor_scalar(out=o[:], in0=src[:], scalar1=sc, scalar2=None, op0=ALU.mult)
            else:
                nc.scalar.activation(out=o[:], in_=src[:], func=ACT.Copy, scale=sc)
            parts[q] = o
            if last:
                nc.sync.dma_start(out=out[P * q : P * (q + 1), :], in_=o[:])

        def run_step(name, eng):
            if name.startswith("dum"):
                if eng == "p":
                    pending.append(name)
            elif name.startswith("st"):
                scale_tr(int(name[2:]))
            elif name.startswith("sev"):
                scale_ev(int(name[3:]), eng)
            elif name == "rowsf":
                par(0)
            elif name == "pt":
                par(1)
            elif name == "cols":
                par(2)
            elif name.startswith("fil"):
                h = int(name[4:])
                f_interleave(int(name[3:4]), eng, 256 * h, 256 * h + 256)
            elif name.startswith("fq"):
                f_quant(int(name[2:]))
            elif name.startswith("prod"):
                prod(int(name[4:5]), int(name[5:]))
            elif name.startswith("ptr"):
                ptr(int(name[3:4]), int(name[4:5]), int(name[5:]))
            elif name.startswith("pev"):
                pev(int(name[3:4]), int(name[4:5]), int(name[5:]), eng)
            elif name.startswith("pq"):
                pq(int(name[2:3]), int(name[3:]))
            elif name.startswith("mx1"):
                mx1(int(name[3:4]), int(name[4:]))
            elif name.startswith("ln"):
                ln(int(name[2:3]), int(name[3:]))
            elif name.startswith("gb"):
                gb(int(name[2:3]), int(name[3:]), eng)
            elif name.startswith("htr"):
                htr(int(name[3:4]), int(name[4:]))
            elif name.startswith("hex"):
                hex_(int(name[3:4]), int(name[4:]))
            elif name.startswith("hq"):
                hq(int(name[2:]))
            elif name.startswith("btr"):
                btr(int(name[3:4]), int(name[4:]))
            elif name.startswith("bev"):
                bev(int(name[3:4]), int(name[4:]), eng)
            elif name.startswith("bq"):
                bq(int(name[2:]))
            elif name.startswith("mx2"):
                mx2(int(name[3:4]), int(name[5:]))
            else:
                assert name.startswith("oev")
                oev(int(name[3:4]), int(name[5:]), eng)

        for step in STEPS.split():
            name, eng = step.split(":")
            run_step(name, eng)
